import numpy as np, ml_dtypes
CORES = [6,14,22,30,38,46,54,62,134,142,150,158,166,174,182,190,262,270,278,286,294,302,310,318,390,398,406,414,422,430,438,446]
N = 32
GROUPS = [[0,8,16,24],[1,9,17,25],[2,10,18,26],[3,11,19,27],[4,12,20,28],[5,13,21,29],[6,14,22,30],[7,15,23,31]]
def setup_inputs(rng):
    return {"x": rng.standard_normal((N, 128, 256), dtype=np.float32).astype(ml_dtypes.bfloat16)}
def reference(x):
    y = np.empty((N, 128, 64), x.dtype)
    for g in GROUPS:
        s = x[g].sum(axis=0, dtype=np.float64).astype(x[g].dtype)
        n = len(g); b = x.shape[2] // n
        for i, r in enumerate(g):
            y[r] = s[:, i * b:(i + 1) * b]
    return {"y": y}

@@ -1,0 +1,52 @@
+from concourse.bass import DstId, RemoteDMATransfer
+from concourse.mybir import AluOpType
+
+B = 64
+
+SCRATCH = {
+    "snd": ("sbuf", [128, 2 * B], "bfloat16"),
+    "keep": ("sbuf", [128, B], "bfloat16"),
+    "lsw": ("sbuf", [128, 2 * B], "bfloat16"),
+    "lcb": ("sbuf", [128, B], "bfloat16"),
+}
+SEMAPHORES = ["ld_snd", "ld_keep", "ld_y", "arr_sw", "arr_cb", "sent", "acc1", "acc2"]
+
+
+def rank_program(g, core, T, topo):
+    rank = T.rank_of(core)
+    if rank is None:
+        return
+    grp = [m for m in T.tables["GROUPS"] if rank in m][0]
+    cores = [T.cores[r] for r in grp]
+    me = grp.index(rank)
+    sw = [i for i in range(4) if i != me and topo.rack(topo.host(cores[i])) == topo.rack(topo.host(core))][0]
+    cb = [i for i in range(4) if i not in (me, sw) and topo.may_write(core, cores[i])][0]
+    dg = [i for i in range(4) if i not in (me, sw, cb)][0]
+    S = T.sem
+
+    def blk(i):
+        return T.x[:, i * B:(i + 1) * B]
+
+    g.sync.dma_start(T.snd[:, 0:B], blk(sw)).then_inc(S.ld_snd, 16)
+    g.scalar.dma_start(T.snd[:, B:2 * B], blk(dg)).then_inc(S.ld_snd, 16)
+    g.sync.dma_start(T.keep[:], blk(cb)).then_inc(S.ld_keep, 16)
+    g.scalar.dma_start(T.y[:], blk(me)).then_inc(S.ld_y, 16)
+
+    rid, pid = topo.addr(cores[sw], core)
+    g.wait_ge(S.ld_snd, 32)
+    g.remote_dma(T.lsw[:], T.snd[:], S.arr_sw, S.sent, pid, rid, topo.mask(core, cores[sw]))
+
+    rid, pid = topo.addr(cores[cb], core)
+    g.wait_ge(S.ld_keep, 16)
+    g.wait_ge(S.arr_sw, 8)
+    g.remote_dma_fused([RemoteDMATransfer(
+        dst_ids=[DstId(rid=rid, pnc=pid)], dma_engine_mask=topo.mask(core, cores[cb]), remote_sem=S.arr_cb,
+        srcs=[T.keep[:], T.lsw[:, B:2 * B]], dsts=[T.lcb[:]], alu_op=1)], local_sem=S.sent)
+
+    g.wait_ge(S.ld_y, 16)
+    g.dma_start(T.y[:], T.lsw[:, 0:B], accum_op=AluOpType.add).then_inc(S.acc1, 16)
+    g.wait_ge(S.acc1, 16)
+    g.wait_ge(S.arr_cb, 8)
+    g.dma_start(T.y[:], T.lcb[:], accum_op=AluOpType.add).then_inc(S.acc2, 16)
+    g.wait_ge(S.acc2, 16)
+    g.wait_ge(S.sent, 16)

@@ -4,12 +4,14 @@ from concourse.mybir import AluOpType
 B = 64
 
 SCRATCH = {
-    "snd": ("sbuf", [128, 2 * B], "bfloat16"),
-    "keep": ("sbuf", [128, B], "bfloat16"),
-    "lsw": ("sbuf", [128, 2 * B], "bfloat16"),
-    "lcb": ("sbuf", [128, B], "bfloat16"),
+    "d_dg": ("dram", [128, B], "bfloat16"),
+    "d_sw": ("dram", [128, B], "bfloat16"),
+    "d_cb": ("dram", [128, B], "bfloat16"),
+    "l_fold": ("dram", [128, B], "bfloat16"),
+    "l_sw": ("dram", [128, B], "bfloat16"),
+    "l_cb": ("dram", [128, B], "bfloat16"),
 }
-SEMAPHORES = ["ld_snd", "ld_keep", "ld_y", "arr_sw", "arr_cb", "sent", "acc1", "acc2"]
+SEMAPHORES = ["ld_dg", "ld_sw", "ld_cb", "ld_y", "arr_fold", "arr_sw", "arr_cb", "sent", "acc1", "acc2"]
 
 
 def rank_program(g, core, T, topo):
@@ -19,34 +21,39 @@ def rank_program(g, core, T, topo):
     grp = [m for m in T.tables["GROUPS"] if rank in m][0]
     cores = [T.cores[r] for r in grp]
     me = grp.index(rank)
-    sw = [i for i in range(4) if i != me and topo.rack(topo.host(cores[i])) == topo.rack(topo.host(core))][0]
-    cb = [i for i in range(4) if i not in (me, sw) and topo.may_write(core, cores[i])][0]
-    dg = [i for i in range(4) if i not in (me, sw, cb)][0]
+    others = [i for i in range(len(grp)) if i != me]
+    sw = [i for i in others if topo.same_plane(core, cores[i])][0]
+    cb = [i for i in others if i != sw and topo.may_write(core, cores[i])][0]
+    dg = [i for i in others if i not in (sw, cb)][0]
     S = T.sem
 
     def blk(i):
         return T.x[:, i * B:(i + 1) * B]
 
-    g.sync.dma_start(T.snd[:, 0:B], blk(sw)).then_inc(S.ld_snd, 16)
-    g.scalar.dma_start(T.snd[:, B:2 * B], blk(dg)).then_inc(S.ld_snd, 16)
-    g.sync.dma_start(T.keep[:], blk(cb)).then_inc(S.ld_keep, 16)
+    g.sync.dma_start(T.d_dg[:], blk(dg)).then_inc(S.ld_dg, 16)
+    g.scalar.dma_start(T.d_cb[:], blk(cb)).then_inc(S.ld_cb, 16)
+    g.sync.dma_start(T.d_sw[:], blk(sw)).then_inc(S.ld_sw, 16)
     g.scalar.dma_start(T.y[:], blk(me)).then_inc(S.ld_y, 16)
 
     rid, pid = topo.addr(cores[sw], core)
-    g.wait_ge(S.ld_snd, 32)
-    g.remote_dma(T.lsw[:], T.snd[:], S.arr_sw, S.sent, pid, rid, topo.mask(core, cores[sw]))
+    m = topo.mask(core, cores[sw])
+    g.wait_ge(S.ld_dg, 16)
+    g.remote_dma(T.l_fold[:], T.d_dg[:], S.arr_fold, S.sent, pid, rid, m)
+    g.wait_ge(S.ld_sw, 16)
+    g.remote_dma(T.l_sw[:], T.d_sw[:], S.arr_sw, S.sent, pid, rid, m)
 
     rid, pid = topo.addr(cores[cb], core)
-    g.wait_ge(S.ld_keep, 16)
-    g.wait_ge(S.arr_sw, 8)
+    g.wait_ge(S.ld_cb, 16)
+    g.wait_ge(S.arr_fold, 8)
     g.remote_dma_fused([RemoteDMATransfer(
         dst_ids=[DstId(rid=rid, pnc=pid)], dma_engine_mask=topo.mask(core, cores[cb]), remote_sem=S.arr_cb,
-        srcs=[T.keep[:], T.lsw[:, B:2 * B]], dsts=[T.lcb[:]], alu_op=1)], local_sem=S.sent)
+        srcs=[T.d_cb[:], T.l_fold[:]], dsts=[T.l_cb[:]], alu_op=1)], local_sem=S.sent)
 
     g.wait_ge(S.ld_y, 16)
-    g.dma_start(T.y[:], T.lsw[:, 0:B], accum_op=AluOpType.add).then_inc(S.acc1, 16)
+    g.wait_ge(S.arr_sw, 8)
+    g.dma_start(T.y[:], T.l_sw[:], accum_op=AluOpType.add, max_dma_last_dim=4096).then_inc(S.acc1, 16)
     g.wait_ge(S.acc1, 16)
     g.wait_ge(S.arr_cb, 8)
-    g.dma_start(T.y[:], T.lcb[:], accum_op=AluOpType.add).then_inc(S.acc2, 16)
+    g.dma_start(T.y[:], T.l_cb[:], accum_op=AluOpType.add, max_dma_last_dim=4096).then_inc(S.acc2, 16)
     g.wait_ge(S.acc2, 16)
-    g.wait_ge(S.sent, 16)
+    g.wait_ge(S.sent, 24)

from concourse.bass import DstId, RemoteDMATransfer
from concourse.mybir import AluOpType

B = 64

SCRATCH = {
    "d_dg": ("dram", [128, B], "bfloat16"),
    "d_sw": ("dram", [128, B], "bfloat16"),
    "d_cb": ("dram", [128, B], "bfloat16"),
    "l_fold": ("dram", [128, B], "bfloat16"),
    "l_sw": ("dram", [128, B], "bfloat16"),
    "l_cb": ("dram", [128, B], "bfloat16"),
}
SEMAPHORES = ["ld_dg", "ld_sw", "ld_cb", "ld_y", "arr_fold", "arr_sw", "arr_cb", "sent", "acc1", "acc2"]


def rank_program(g, core, T, topo):
    rank = T.rank_of(core)
    if rank is None:
        return
    grp = [m for m in T.tables["GROUPS"] if rank in m][0]
    cores = [T.cores[r] for r in grp]
    me = grp.index(rank)
    others = [i for i in range(len(grp)) if i != me]
    sw = [i for i in others if topo.same_plane(core, cores[i])][0]
    cb = [i for i in others if i != sw and topo.may_write(core, cores[i])][0]
    dg = [i for i in others if i not in (sw, cb)][0]
    S = T.sem

    def blk(i):
        return T.x[:, i * B:(i + 1) * B]

    g.sync.dma_start(T.d_dg[:], blk(dg)).then_inc(S.ld_dg, 16)
    g.scalar.dma_start(T.d_cb[:], blk(cb)).then_inc(S.ld_cb, 16)
    g.sync.dma_start(T.d_sw[:], blk(sw)).then_inc(S.ld_sw, 16)
    g.scalar.dma_start(T.y[:], blk(me)).then_inc(S.ld_y, 16)

    rid, pid = topo.addr(cores[sw], core)
    m = topo.mask(core, cores[sw])
    g.wait_ge(S.ld_dg, 16)
    g.remote_dma(T.l_fold[:], T.d_dg[:], S.arr_fold, S.sent, pid, rid, m)
    g.wait_ge(S.ld_sw, 16)
    g.remote_dma(T.l_sw[:], T.d_sw[:], S.arr_sw, S.sent, pid, rid, m)

    rid, pid = topo.addr(cores[cb], core)
    g.wait_ge(S.ld_cb, 16)
    g.wait_ge(S.arr_fold, 8)
    g.remote_dma_fused([RemoteDMATransfer(
        dst_ids=[DstId(rid=rid, pnc=pid)], dma_engine_mask=topo.mask(core, cores[cb]), remote_sem=S.arr_cb,
        srcs=[T.d_cb[:], T.l_fold[:]], dsts=[T.l_cb[:]], alu_op=1)], local_sem=S.sent)

    g.wait_ge(S.ld_y, 16)
    g.wait_ge(S.arr_sw, 8)
    g.dma_start(T.y[:], T.l_sw[:], accum_op=AluOpType.add, max_dma_last_dim=4096).then_inc(S.acc1, 16)
    g.wait_ge(S.acc1, 16)
    g.wait_ge(S.arr_cb, 8)
    g.dma_start(T.y[:], T.l_cb[:], accum_op=AluOpType.add, max_dma_last_dim=4096).then_inc(S.acc2, 16)
    g.wait_ge(S.acc2, 16)
    g.wait_ge(S.sent, 24)
